import numpy as np
import ml_dtypes


def mxq(x, axis, fmt="e4m3"):
    dtype, down = {"e4m3": (ml_dtypes.float8_e4m3fn, 7), "e5m2": (ml_dtypes.float8_e5m2, 14)}[fmt]
    v = np.moveaxis(np.asarray(x, np.float32).astype(ml_dtypes.bfloat16).astype(np.float64), axis, -1)
    blocks = v.reshape(v.shape[:-1] + (-1, 32))
    amax = np.abs(blocks).max(-1, keepdims=True)
    byte = np.maximum(np.where(amax > 0, np.frexp(amax)[1] - 1 + 127, 0) - down, 1)
    scale = np.exp2(byte - 127.0)
    codes = (blocks / scale).astype(np.float32).astype(dtype).astype(np.float64)
    return np.moveaxis((codes * scale).reshape(v.shape), -1, axis)


WIDE = False


def mx_kscale(k):
    if not WIDE:
        return np.ones(k)
    levels = np.array([10, -10, 5, -5, 0])
    if k % 512:
        return np.exp2(np.random.permutation(np.resize(levels, k // 32))).repeat(32)
    a = np.empty((k // 512, 16))
    for p in range(k // 512):
        a[p, :8] = np.random.permutation(np.resize(levels, 8))
        for g in range(8):
            far = levels[np.abs(levels - a[p, g]) >= 10]
            a[p, g + 8] = far[np.random.randint(len(far))]
    return np.exp2(a.ravel()).repeat(32)


def f64(x):
    return np.asarray(x).astype(np.float64)


def striped(idx):
    return np.tile(idx.reshape(-1, 16).T, (8, 1)).astype(np.uint16)


def unstriped(offs):
    return offs[:16].T.reshape(-1).astype(np.int64)


def pack_weight(w):
    k, n = w.shape
    w = f64(np.asarray(w, np.float32).astype(ml_dtypes.bfloat16)).reshape(k // 32, 32, n)
    amax = np.abs(w).max(1)
    byte = np.clip(np.where(amax > 0, np.frexp(amax)[1] - 1 + 127 - 7, 1), 1, 254)
    scaled = (w * np.exp2(127.0 - byte)[:, None, :]).reshape(k, n).astype(np.float32)
    words = np.ascontiguousarray(scaled.reshape(k // 512, 128, 4, n).transpose(0, 1, 3, 2)).astype(ml_dtypes.float8_e4m3fn).view(np.uint8)
    return words, np.ascontiguousarray(byte.astype(np.uint8).reshape(k // 512, 16, n))


def unpack_weight(words, scales):
    g, p, n, _ = words.shape
    vals = np.ascontiguousarray(words).view(ml_dtypes.float8_e4m3fn).astype(np.float64) * np.repeat(np.exp2(scales.astype(np.float64) - 127.0), 8, axis=1)[..., None]
    return vals.transpose(0, 1, 3, 2).reshape(g * 512, n)


def sigmoid(v):
    return 1.0 / (1.0 + np.exp(-np.maximum(v, -700.0)))


K, T, S, N, H, W = 512, 2048, 512, 512, 512, 2048


def setup_inputs():
    n = np.random.standard_normal
    s = mx_kscale(K)[:, None]
    u = mx_kscale(H)
    packed_xT = pack_weight(n((K, T)) * s)
    return {
        "x_words": packed_xT[0],
        "x_scales": packed_xT[1],
        "w1": (n((K, H)) / np.sqrt(K) / s).astype(np.float32),
        "gn": (np.random.uniform(0.5, 1.5, (H, 1)) * u[:, None]).astype(np.float32),
        "w2": (n((H, N)) / np.sqrt(2 * H) / u[:, None]).astype(np.float32),
        "w3": (n((K, N)) / np.sqrt(2 * K) / s).astype(np.float32),
        "offs": striped(np.random.permutation(T)[:S]),
        "n1": striped(np.random.permutation(S)),
        "n2": striped(np.random.permutation(S)),
        "two": striped(np.random.permutation(T)[:S]),
        "n3": striped(np.random.randint(0, S, W)),
    }


def reference(x_words, x_scales, w1, gn, w2, w3, offs, n1, n2, two, n3):
    xq = unpack_weight(x_words, x_scales)[:, unstriped(offs)]
    y = mxq(f64(w1), 0, "e4m3").T @ xq
    st = y * (sigmoid(y[:, unstriped(n1)]))
    z = f64(gn) * (st - st[:, unstriped(n2)])
    x_two = unpack_weight(x_words, x_scales)[:, unstriped(two)]
    h = mxq(f64(w2), 0, "e4m3").T @ mxq(z, 0, "e4m3") + mxq(f64(w3), 0, "e4m3").T @ x_two
    mb = h[:, unstriped(n3)]
    mx = mb.reshape(N, S, 4).max(axis=2)
    mn = mb.reshape(N, S, 4).min(axis=2)
    return mx * np.tanh(h - mn)

@@ -1,0 +1,261 @@
+from contextlib import ExitStack
+
+import concourse.mybir as mybir
+
+K, T, S, N, H, W = 512, 2048, 512, 512, 512, 2048
+FLOPS = 3 * 2 * 512 * 512 * 512
+
+F32 = mybir.dt.float32
+BF16 = mybir.dt.bfloat16
+I32 = mybir.dt.int32
+U32 = mybir.dt.uint32
+U16 = mybir.dt.uint16
+U8 = mybir.dt.uint8
+FP8X4 = mybir.dt.float8_e4m3fn_x4
+ALU = mybir.AluOpType
+ACT = mybir.ActivationFunctionType
+
+P = 128
+PACK = 4
+SPARE = 16
+HALF = S // 2
+GROUP = 4
+CHUNK = 512
+
+
+def tile_picked_mixinhopggtan_none_p_kernel(
+    tc, x_words, x_scales, w1, gn, w2, w3, offs, n1, n2, two, n3, out
+):
+    nc = tc.nc
+    with ExitStack() as ctx:
+        keep = ctx.enter_context(tc.tile_pool(name="keep", bufs=1))
+        ring = ctx.enter_context(tc.tile_pool(name="ring", bufs=2))
+        psum = ctx.enter_context(tc.psum_pool(name="psum", bufs=1))
+
+        def load_list(name, src):
+            tile = keep.tile(list(src.shape), U16, name=name)
+            nc.sync.dma_start(out=tile[:], in_=src)
+            return tile
+
+        xs = keep.tile([P, T], U8, name="xs", align_bytes=64)
+        nc.vector.memset(xs[:].bitcast(I32), 0)
+        offs_t = load_list("offs_t", offs)
+        two_t = load_list("two_t", two)
+        for q in range(4):
+            nc.sync.dma_start(
+                out=xs[32 * q : 32 * q + 4, :].bitcast(I32),
+                in_=x_scales[0, 4 * q : 4 * q + 4, :].bitcast(I32),
+            )
+        xw = keep.tile([P, T], U32, name="xw", align_bytes=64)
+        nc.sync.dma_start(
+            out=xw[:].bitcast(I32),
+            in_=x_words[0].rearrange("p n r -> p (n r)").bitcast(I32),
+        )
+        w1_rows = w1.rearrange("(p j) c -> p j c", j=PACK)
+        w1_raw = []
+        for a in range(2):
+            raw = keep.tile([P, PACK, H // 2], F32, name="w1_raw%d" % a)
+            nc.sync.dma_start(out=raw[:], in_=w1_rows[:, :, a * (H // 2) : (a + 1) * (H // 2)])
+            w1_raw.append(raw)
+        n1_t = load_list("n1_t", n1)
+        gn_t = keep.tile([P, PACK], F32, name="gn_t")
+        nc.sync.dma_start(out=gn_t[:], in_=gn.rearrange("(p t) o -> p (t o)", t=PACK))
+        w3_raw = keep.tile([P, PACK, N], F32, name="w3_raw")
+        nc.sync.dma_start(out=w3_raw[:], in_=w3.rearrange("(p j) c -> p j c", j=PACK))
+        n2_t = load_list("n2_t", n2)
+        w2_raw = keep.tile([P, PACK, N], F32, name="w2_raw")
+        nc.sync.dma_start(out=w2_raw[:], in_=w2.rearrange("(p j) c -> p j c", j=PACK))
+        n3_t = load_list("n3_t", n3)
+
+        h_sb = [keep.tile([P, S + SPARE], F32, name="h_sb%d" % u) for u in range(4)]
+        for u in range(4):
+            nc.gpsimd.memset(h_sb[u][:, S:], 0.0)
+
+        def pick(name, window, offsets, dtype):
+            tile = keep.tile([P, S], dtype, name=name, align_bytes=64)
+            nc.vector.tensor_copy(out=tile[:], in_=window[:].indirect(offsets[:]))
+            return tile
+
+        xq_scales = pick("xq_scales", xs, offs_t, U8)
+        x2_scales = pick("x2_scales", xs, two_t, U8)
+        xq_words = pick("xq_words", xw, offs_t, U32)
+
+        w1_b = keep.tile([P, PACK, P, PACK], BF16, name="w1_b", align_bytes=64)
+        w1_view = w1_b[:].rearrange("p t m j -> p m j t")
+        nc.scalar.copy(
+            out=w1_view[:, 0 : P // 2], in_=w1_raw[0][:].rearrange("p j (m t) -> p m j t", t=PACK)
+        )
+        x2_words = pick("x2_words", xw, two_t, U32)
+        nc.vector.tensor_copy(
+            out=w1_view[:, P // 2 : P], in_=w1_raw[1][:].rearrange("p j (m t) -> p m j t", t=PACK)
+        )
+        w1_codes = keep.tile([P, H], U32, name="w1_codes", align_bytes=64)
+        w1_scales = keep.tile([P, H], U8, name="w1_scales", align_bytes=64)
+        y_ps = [psum.tile([P, S], F32, name="y_ps%d" % t, tag="y_ps%d" % t) for t in range(PACK)]
+        for t in range(PACK):
+            cols = slice(t * P, (t + 1) * P)
+            nc.vector.quantize_mx(
+                out=w1_codes[:, cols].bitcast(FP8X4),
+                scales=w1_scales[:, cols],
+                in_=w1_b[:, t].rearrange("p m j -> p (m j)"),
+            )
+            nc.tensor.matmul_mx(
+                out=y_ps[t][:],
+                lhsT=w1_codes[:, cols].bitcast(FP8X4),
+                lhsT_scale=w1_scales[:, cols],
+                rhs=xq_words[:].bitcast(FP8X4),
+                rhs_scale=xq_scales[:],
+                start=True,
+                stop=True,
+            )
+
+        def cast_weight(name, raw):
+            tile = keep.tile([P, N, PACK], BF16, name=name, tag=name, align_bytes=64)
+            nc.vector.tensor_copy(
+                out=tile[:].rearrange("p (c i) j -> p c j i", i=4),
+                in_=raw[:].rearrange("p j (c i) -> p c j i", i=4),
+            )
+            return tile
+
+        def quantise_weight(name, grouped):
+            codes = keep.tile([P, N], U32, name=name + "_codes", align_bytes=64)
+            scales = keep.tile([P, N], U8, name=name + "_scales", align_bytes=64)
+            nc.vector.quantize_mx(
+                out=codes[:].bitcast(FP8X4), scales=scales[:], in_=grouped[:].rearrange("p c j -> p (c j)")
+            )
+            return codes, scales
+
+        st = keep.tile([P, PACK, S], F32, name="st")
+        y_sb = [keep.tile([P, S], F32, name="y_sb%d" % t) for t in range(PACK)]
+        gate = [keep.tile([P, S], F32, name="gate%d" % t, tag="gate%d" % t) for t in range(PACK)]
+
+        def gates(t):
+            for a in range(2):
+                nc.scalar.activation(
+                    out=gate[t][:, a * HALF : (a + 1) * HALF],
+                    in_=y_sb[t][:].indirect(n1_t[:, a * 16 : (a + 1) * 16]),
+                    func=ACT.Sigmoid,
+                )
+
+        def make_st(t):
+            nc.vector.scalar_tensor_tensor(
+                out=st[:, t, :], in0=y_ps[t][:], scalar=gn_t[:, t : t + 1], in1=gate[t][:],
+                op0=ALU.mult, op1=ALU.mult,
+            )
+
+        for t in range(PACK):
+            nc.vector.tensor_copy(out=y_sb[t][:], in_=y_ps[t][:])
+            gates(t)
+        make_st(0)
+        w3_b = cast_weight("w3_b", w3_raw)
+        make_st(1)
+        w3_codes, w3_scales = quantise_weight("w3", w3_b)
+        make_st(2)
+        make_st(3)
+        w2_b = cast_weight("w2_b", w2_raw)
+        w2_codes, w2_scales = quantise_weight("w2", w2_b)
+
+        z_codes = keep.tile([P, S], U32, name="z_codes", align_bytes=64)
+        z_scales = keep.tile([P, S], U8, name="z_scales", align_bytes=64)
+        h_ps = []
+        for a in range(2):
+            cols = slice(a * HALF, (a + 1) * HALF)
+            banks = [
+                psum.tile([P, HALF], F32, name="h_ps%d_%d" % (a, u), tag=("h_ps%d", "y_ps%d")[a] % u)
+                for u in range(4)
+            ]
+            h_ps.append(banks)
+            for u in range(4):
+                wc = slice(u * P, (u + 1) * P)
+                nc.tensor.matmul_mx(
+                    out=banks[u][:],
+                    lhsT=w3_codes[:, wc].bitcast(FP8X4),
+                    lhsT_scale=w3_scales[:, wc],
+                    rhs=x2_words[:, cols].bitcast(FP8X4),
+                    rhs_scale=x2_scales[:, cols],
+                    start=True,
+                    stop=False,
+                )
+            other = keep.tile([P, PACK, HALF], F32, name="other%d" % a, tag=("other0", "gate3")[a])
+            for t in range(PACK):
+                src = st[:, t, :].indirect(n2_t[:, a * 16 : (a + 1) * 16])
+                if (a, t) == (1, 0):
+                    nc.vector.tensor_copy(out=other[:, t, :], in_=src)
+                else:
+                    nc.scalar.activation(out=other[:, t, :], in_=src, func=ACT.Copy)
+            z_b = keep.tile([P, HALF, PACK], BF16, name="z_b%d" % a, tag="w2_b", align_bytes=64)
+            nc.vector.tensor_tensor(
+                out=z_b[:].rearrange("p (c i) t -> p c t i", i=4),
+                in0=st[:, :, cols].rearrange("p t (c i) -> p c t i", i=4),
+                in1=other[:].rearrange("p t (c i) -> p c t i", i=4),
+                op=ALU.subtract,
+            )
+            nc.vector.quantize_mx(
+                out=z_codes[:, cols].bitcast(FP8X4),
+                scales=z_scales[:, cols],
+                in_=z_b[:].rearrange("p c t -> p (c t)"),
+            )
+            for u in range(4):
+                wc = slice(u * P, (u + 1) * P)
+                nc.tensor.matmul_mx(
+                    out=banks[u][:],
+                    lhsT=w2_codes[:, wc].bitcast(FP8X4),
+                    lhsT_scale=w2_scales[:, wc],
+                    rhs=z_codes[:, cols].bitcast(FP8X4),
+                    rhs_scale=z_scales[:, cols],
+                    start=False,
+                    stop=True,
+                )
+        for u in range(4):
+            nc.scalar.copy(out=h_sb[u][:, 0:HALF], in_=h_ps[0][u][:])
+
+        per = CHUNK // GROUP
+
+        def copy_h(u, engine_copy):
+            engine_copy(out=h_sb[u][:, HALF:S], in_=h_ps[1][u][:])
+
+        def finish(u, c0, c1, tag):
+            res = keep.tile([P, c1 - c0], F32, name="res%d_%d" % (u, c0), tag=tag)
+            nc.vector.tensor_tensor(out=res[:], in0=mx[u][:, c0:c1], in1=th[u][:, c0:c1], op=ALU.mult)
+            nc.sync.dma_start(out=out[u * P : (u + 1) * P, c0:c1], in_=res[:])
+
+        mx = [keep.tile([P, S], F32, name="mx%d" % u) for u in range(4)]
+        th = [keep.tile([P, S], F32, name="th%d" % u) for u in range(4)]
+        copy_h(0, nc.vector.tensor_copy)
+        copy_h(1, nc.scalar.copy)
+        for u in range(4):
+            mb = keep.tile([P, S, GROUP], F32, name="mb%d" % u, tag="mb%d" % u)
+            for g in range(4):
+                dst = mb[:, g * per : (g + 1) * per, :].rearrange("p j t -> p (j t)")
+                src = h_sb[u][:].indirect(n3_t[:, g * 32 : (g + 1) * 32])
+                if u == 0 and g in (0, 2):
+                    nc.vector.tensor_copy(out=dst, in_=src)
+                else:
+                    nc.scalar.activation(out=dst, in_=src, func=ACT.Copy)
+            parts = [(0, 512)] if u < 3 else [(0, 256), (256, 384), (384, 512)]
+            for c0, c1 in parts:
+                n = c1 - c0
+                lo2 = ring.tile([P, n, 2], F32, name="lo2")
+                hi2 = ring.tile([P, n, 2], F32, name="hi2")
+                for b0 in range(0, n, HALF):
+                    b1 = min(n, b0 + HALF)
+                    src = mb[:, c0 + b0 : c0 + b1, :]
+                    nc.vector.tensor_tensor(out=lo2[:, b0:b1, :], in0=src[:, :, 0:2], in1=src[:, :, 2:4], op=ALU.min)
+                    nc.vector.tensor_tensor(out=hi2[:, b0:b1, :], in0=src[:, :, 0:2], in1=src[:, :, 2:4], op=ALU.max)
+                mn_tag = "mn%d_%d" % (u, c0)
+                mn = keep.tile([P, n], F32, name=mn_tag, tag=mn_tag)
+                nc.vector.tensor_tensor(out=mn[:], in0=lo2[:, :, 0], in1=lo2[:, :, 1], op=ALU.min)
+                nc.vector.tensor_tensor(out=mx[u][:, c0:c1], in0=hi2[:, :, 0], in1=hi2[:, :, 1], op=ALU.max)
+                diff_tag = "mb%d" % (u + 2) if u < 2 else "diff%d_%d" % (u, c0)
+                diff = keep.tile([P, n], F32, name="diff%d_%d" % (u, c0), tag=diff_tag)
+                nc.vector.tensor_tensor(out=diff[:], in0=h_sb[u][:, c0:c1], in1=mn[:], op=ALU.subtract)
+                nc.scalar.activation(out=th[u][:, c0:c1], in_=diff[:], func=ACT.Tanh)
+                if u in (1, 2):
+                    finish(u - 1, 0, S, mn_tag)
+                elif (u, c0) == (3, 256):
+                    finish(2, 0, S, mn_tag)
+                elif (u, c0) == (3, 384):
+                    finish(3, 0, 384, mn_tag)
+                    finish(3, 384, S, "res_last")
+            if u < 2:
+                copy_h(u + 2, nc.vector.tensor_copy)

@@ -38,14 +38,13 @@ def tile_picked_mixinhopggtan_none_p_kernel(
             return tile
 
         xs = keep.tile([P, T], U8, name="xs", align_bytes=64)
-        nc.vector.memset(xs[:].bitcast(I32), 0)
         offs_t = load_list("offs_t", offs)
-        two_t = load_list("two_t", two)
         for q in range(4):
             nc.sync.dma_start(
-                out=xs[32 * q : 32 * q + 4, :].bitcast(I32),
-                in_=x_scales[0, 4 * q : 4 * q + 4, :].bitcast(I32),
+                out=xs[32 * q : 32 * q + 32, :].bitcast(I32),
+                in_=x_scales[0, 4 * q : 4 * q + 4, :].bitcast(I32).unsqueeze(0).broadcast_to([8, 4, T // 4]),
             )
+        two_t = load_list("two_t", two)
         xw = keep.tile([P, T], U32, name="xw", align_bytes=64)
         nc.sync.dma_start(
             out=xw[:].bitcast(I32),
@@ -60,19 +59,19 @@ def tile_picked_mixinhopggtan_none_p_kernel(
         n1_t = load_list("n1_t", n1)
         gn_t = keep.tile([P, PACK], F32, name="gn_t")
         nc.sync.dma_start(out=gn_t[:], in_=gn.rearrange("(p t) o -> p (t o)", t=PACK))
-        w3_raw = keep.tile([P, PACK, N], F32, name="w3_raw")
+        w3_raw = keep.tile([P, PACK, N], F32, name="w3_raw", tag="w3_raw")
         nc.sync.dma_start(out=w3_raw[:], in_=w3.rearrange("(p j) c -> p j c", j=PACK))
         n2_t = load_list("n2_t", n2)
         w2_raw = keep.tile([P, PACK, N], F32, name="w2_raw")
         nc.sync.dma_start(out=w2_raw[:], in_=w2.rearrange("(p j) c -> p j c", j=PACK))
         n3_t = load_list("n3_t", n3)
 
-        h_sb = [keep.tile([P, S + SPARE], F32, name="h_sb%d" % u) for u in range(4)]
+        h_sb = [keep.tile([P, 2 * S + SPARE], F32, name="h_sb%d" % u) for u in range(4)]
         for u in range(4):
             nc.gpsimd.memset(h_sb[u][:, S:], 0.0)
 
-        def pick(name, window, offsets, dtype):
-            tile = keep.tile([P, S], dtype, name=name, align_bytes=64)
+        def pick(name, window, offsets, dtype, tag=None):
+            tile = keep.tile([P, S], dtype, name=name, tag=tag or name, align_bytes=64)
             nc.vector.tensor_copy(out=tile[:], in_=window[:].indirect(offsets[:]))
             return tile
 
@@ -80,7 +79,7 @@ def tile_picked_mixinhopggtan_none_p_kernel(
         x2_scales = pick("x2_scales", xs, two_t, U8)
         xq_words = pick("xq_words", xw, offs_t, U32)
 
-        w1_b = keep.tile([P, PACK, P, PACK], BF16, name="w1_b", align_bytes=64)
+        w1_b = keep.tile([P, PACK, P, PACK], BF16, name="w1_b", tag="w1_b", align_bytes=64)
         w1_view = w1_b[:].rearrange("p t m j -> p m j t")
         nc.scalar.copy(
             out=w1_view[:, 0 : P // 2], in_=w1_raw[0][:].rearrange("p j (m t) -> p m j t", t=PACK)
@@ -92,13 +91,15 @@ def tile_picked_mixinhopggtan_none_p_kernel(
         w1_codes = keep.tile([P, H], U32, name="w1_codes", align_bytes=64)
         w1_scales = keep.tile([P, H], U8, name="w1_scales", align_bytes=64)
         y_ps = [psum.tile([P, S], F32, name="y_ps%d" % t, tag="y_ps%d" % t) for t in range(PACK)]
-        for t in range(PACK):
-            cols = slice(t * P, (t + 1) * P)
+        for t0, t1 in ((0, 1), (1, PACK)):
+            cols = slice(t0 * P, t1 * P)
             nc.vector.quantize_mx(
                 out=w1_codes[:, cols].bitcast(FP8X4),
                 scales=w1_scales[:, cols],
-                in_=w1_b[:, t].rearrange("p m j -> p (m j)"),
+                in_=w1_b[:, t0:t1].rearrange("p t m j -> p (t m j)"),
             )
+        for t in range(PACK):
+            cols = slice(t * P, (t + 1) * P)
             nc.tensor.matmul_mx(
                 out=y_ps[t][:],
                 lhsT=w1_codes[:, cols].bitcast(FP8X4),
@@ -109,8 +110,8 @@ def tile_picked_mixinhopggtan_none_p_kernel(
                 stop=True,
             )
 
-        def cast_weight(name, raw):
-            tile = keep.tile([P, N, PACK], BF16, name=name, tag=name, align_bytes=64)
+        def cast_weight(name, raw, tag):
+            tile = keep.tile([P, N, PACK], BF16, name=name, tag=tag, align_bytes=64)
             nc.vector.tensor_copy(
                 out=tile[:].rearrange("p (c i) j -> p c j i", i=4),
                 in_=raw[:].rearrange("p j (c i) -> p c j i", i=4),
@@ -125,34 +126,19 @@ def tile_picked_mixinhopggtan_none_p_kernel(
             )
             return codes, scales
 
-        st = keep.tile([P, PACK, S], F32, name="st")
-        y_sb = [keep.tile([P, S], F32, name="y_sb%d" % t) for t in range(PACK)]
-        gate = [keep.tile([P, S], F32, name="gate%d" % t, tag="gate%d" % t) for t in range(PACK)]
-
-        def gates(t):
-            for a in range(2):
-                nc.scalar.activation(
-                    out=gate[t][:, a * HALF : (a + 1) * HALF],
-                    in_=y_sb[t][:].indirect(n1_t[:, a * 16 : (a + 1) * 16]),
-                    func=ACT.Sigmoid,
-                )
-
-        def make_st(t):
-            nc.vector.scalar_tensor_tensor(
-                out=st[:, t, :], in0=y_ps[t][:], scalar=gn_t[:, t : t + 1], in1=gate[t][:],
-                op0=ALU.mult, op1=ALU.mult,
-            )
-
+        sig = [keep.tile([P, S + SPARE], F32, name="sig%d" % t) for t in range(PACK)]
         for t in range(PACK):
-            nc.vector.tensor_copy(out=y_sb[t][:], in_=y_ps[t][:])
-            gates(t)
-        make_st(0)
-        w3_b = cast_weight("w3_b", w3_raw)
-        make_st(1)
-        w3_codes, w3_scales = quantise_weight("w3", w3_b)
-        make_st(2)
-        make_st(3)
-        w2_b = cast_weight("w2_b", w2_raw)
+            nc.gpsimd.memset(sig[t][:, S:], 0.0)
+        w3_b = cast_weight("w3_b", w3_raw, "w3_b")
+        st = keep.tile([P, PACK, S], F32, name="st", tag="w3_raw")
+        for t in range(PACK):
+            nc.scalar.activation(out=sig[t][:, 0:S], in_=y_ps[t][:], func=ACT.Sigmoid)
+            y_gain = keep.tile([P, S], F32, name="y_gain%d" % t, tag="y_gain%d" % t, align_bytes=64)
+            nc.scalar.activation(out=y_gain[:], in_=y_ps[t][:], func=ACT.Copy, scale=gn_t[:, t : t + 1])
+            nc.vector.tensor_tensor(out=st[:, t, :], in0=sig[t][:].indirect(n1_t[:]), in1=y_gain[:], op=ALU.mult)
+            if t == 0:
+                w3_codes, w3_scales = quantise_weight("w3", w3_b)
+        w2_b = cast_weight("w2_b", w2_raw, "y_gain3")
         w2_codes, w2_scales = quantise_weight("w2", w2_b)
 
         z_codes = keep.tile([P, S], U32, name="z_codes", align_bytes=64)
@@ -176,36 +162,37 @@ def tile_picked_mixinhopggtan_none_p_kernel(
                     start=True,
                     stop=False,
                 )
-            other = keep.tile([P, PACK, HALF], F32, name="other%d" % a, tag=("other0", "gate3")[a])
-            for t in range(PACK):
-                src = st[:, t, :].indirect(n2_t[:, a * 16 : (a + 1) * 16])
-                if (a, t) == (1, 0):
-                    nc.vector.tensor_copy(out=other[:, t, :], in_=src)
-                else:
-                    nc.scalar.activation(out=other[:, t, :], in_=src, func=ACT.Copy)
-            z_b = keep.tile([P, HALF, PACK], BF16, name="z_b%d" % a, tag="w2_b", align_bytes=64)
-            nc.vector.tensor_tensor(
-                out=z_b[:].rearrange("p (c i) t -> p c t i", i=4),
-                in0=st[:, :, cols].rearrange("p t (c i) -> p c t i", i=4),
-                in1=other[:].rearrange("p t (c i) -> p c t i", i=4),
-                op=ALU.subtract,
-            )
-            nc.vector.quantize_mx(
-                out=z_codes[:, cols].bitcast(FP8X4),
-                scales=z_scales[:, cols],
-                in_=z_b[:].rearrange("p c t -> p (c t)"),
-            )
-            for u in range(4):
-                wc = slice(u * P, (u + 1) * P)
-                nc.tensor.matmul_mx(
-                    out=banks[u][:],
-                    lhsT=w2_codes[:, wc].bitcast(FP8X4),
-                    lhsT_scale=w2_scales[:, wc],
-                    rhs=z_codes[:, cols].bitcast(FP8X4),
-                    rhs_scale=z_scales[:, cols],
-                    start=False,
-                    stop=True,
+            other = keep.tile([P, PACK * HALF], F32, name="other%d" % a)
+            for b0, b1 in [(0, HALF)]:
+                n = b1 - b0
+                c0 = a * HALF + b0
+                part = other[:, PACK * b0 : PACK * b1].rearrange("p (t c) -> p t c", t=PACK)
+                for t in range(PACK):
+                    src = st[:, t, :].indirect(n2_t[:, c0 // 16 : (c0 + n) // 16])
+                    nc.scalar.activation(out=part[:, t, :], in_=src, func=ACT.Copy)
+                z_b = keep.tile([P, n, PACK], BF16, name="z_b%d" % c0, tag="y_gain3", align_bytes=64)
+                nc.vector.tensor_tensor(
+                    out=z_b[:].rearrange("p (c i) t -> p c t i", i=4),
+                    in0=st[:, :, c0 : c0 + n].rearrange("p t (c i) -> p c t i", i=4),
+                    in1=part.rearrange("p t (c i) -> p c t i", i=4),
+                    op=ALU.subtract,
                 )
+                nc.vector.quantize_mx(
+                    out=z_codes[:, c0 : c0 + n].bitcast(FP8X4),
+                    scales=z_scales[:, c0 : c0 + n],
+                    in_=z_b[:].rearrange("p c t -> p (c t)"),
+                )
+                for u in range(4):
+                    wc = slice(u * P, (u + 1) * P)
+                    nc.tensor.matmul_mx(
+                        out=banks[u][:, b0:b1],
+                        lhsT=w2_codes[:, wc].bitcast(FP8X4),
+                        lhsT_scale=w2_scales[:, wc],
+                        rhs=z_codes[:, c0 : c0 + n].bitcast(FP8X4),
+                        rhs_scale=z_scales[:, c0 : c0 + n],
+                        start=False,
+                        stop=(b1 == HALF),
+                    )
         for u in range(4):
             nc.scalar.copy(out=h_sb[u][:, 0:HALF], in_=h_ps[0][u][:])
 
@@ -225,9 +212,10 @@ def tile_picked_mixinhopggtan_none_p_kernel(
         copy_h(1, nc.scalar.copy)
         for u in range(4):
             mb = keep.tile([P, S, GROUP], F32, name="mb%d" % u, tag="mb%d" % u)
-            for g in range(4):
-                dst = mb[:, g * per : (g + 1) * per, :].rearrange("p j t -> p (j t)")
-                src = h_sb[u][:].indirect(n3_t[:, g * 32 : (g + 1) * 32])
+            runs = ([(0, 1), (1, 2), (2, 3), (3, 4)], [(0, 2), (2, 4)], [(0, 2), (2, 4)], [(0, 2), (2, 3), (3, 4)])[u]
+            for g, g1 in runs:
+                dst = mb[:, g * per : g1 * per, :].rearrange("p j t -> p (j t)")
+                src = h_sb[u][:].indirect(n3_t[:, g * 32 : g1 * 32])
                 if u == 0 and g in (0, 2):
                     nc.vector.tensor_copy(out=dst, in_=src)
                 else:
@@ -237,8 +225,9 @@ def tile_picked_mixinhopggtan_none_p_kernel(
                 n = c1 - c0
                 lo2 = ring.tile([P, n, 2], F32, name="lo2")
                 hi2 = ring.tile([P, n, 2], F32, name="hi2")
-                for b0 in range(0, n, HALF):
-                    b1 = min(n, b0 + HALF)
+                step = min(n, HALF)
+                for b0 in range(0, n, step):
+                    b1 = b0 + step
                     src = mb[:, c0 + b0 : c0 + b1, :]
                     nc.vector.tensor_tensor(out=lo2[:, b0:b1, :], in0=src[:, :, 0:2], in1=src[:, :, 2:4], op=ALU.min)
                     nc.vector.tensor_tensor(out=hi2[:, b0:b1, :], in0=src[:, :, 0:2], in1=src[:, :, 2:4], op=ALU.max)
@@ -258,4 +247,4 @@ def tile_picked_mixinhopggtan_none_p_kernel(
                     finish(3, 0, 384, mn_tag)
                     finish(3, 384, S, "res_last")
             if u < 2:
-                copy_h(u + 2, nc.vector.tensor_copy)
+                copy_h(u + 2, nc.scalar.copy)

@@ -71,20 +71,20 @@ def tile_picked_mixinhopggtan_none_p_kernel(
             nc.gpsimd.memset(h_sb[u][:, S:], 0.0)
 
         def pick(name, window, offsets, dtype, tag=None):
-            tile = keep.tile([P, S], dtype, name=name, tag=tag or name, align_bytes=64)
-            nc.vector.tensor_copy(out=tile[:], in_=window[:].indirect(offsets[:]))
+            tile = keep.tile([P, offsets.shape[1] * 16], dtype, name=name, tag=tag or name, align_bytes=64)
+            nc.vector.tensor_copy(out=tile[:], in_=window[:].indirect(offsets))
             return tile
 
-        xq_scales = pick("xq_scales", xs, offs_t, U8)
-        x2_scales = pick("x2_scales", xs, two_t, U8)
-        xq_words = pick("xq_words", xw, offs_t, U32)
+        xq_scales = pick("xq_scales", xs, offs_t[:], U8)
+        x2_scales = pick("x2_scales", xs, two_t[:], U8)
+        xq_words = pick("xq_words", xw, offs_t[:], U32)
 
         w1_b = keep.tile([P, PACK, P, PACK], BF16, name="w1_b", tag="w1_b", align_bytes=64)
         w1_view = w1_b[:].rearrange("p t m j -> p m j t")
         nc.scalar.copy(
             out=w1_view[:, 0 : P // 2], in_=w1_raw[0][:].rearrange("p j (m t) -> p m j t", t=PACK)
         )
-        x2_words = pick("x2_words", xw, two_t, U32)
+        x2_words = [pick("x2_words0", xw, two_t[:, 0:16], U32)]
         nc.vector.tensor_copy(
             out=w1_view[:, P // 2 : P], in_=w1_raw[1][:].rearrange("p j (m t) -> p m j t", t=PACK)
         )
@@ -98,6 +98,7 @@ def tile_picked_mixinhopggtan_none_p_kernel(
                 scales=w1_scales[:, cols],
                 in_=w1_b[:, t0:t1].rearrange("p t m j -> p (t m j)"),
             )
+        x2_words.append(pick("x2_words1", xw, two_t[:, 16:32], U32, tag="w1_b"))
         for t in range(PACK):
             cols = slice(t * P, (t + 1) * P)
             nc.tensor.matmul_mx(
@@ -113,13 +114,13 @@ def tile_picked_mixinhopggtan_none_p_kernel(
         def cast_weight(name, raw, tag):
             tile = keep.tile([P, N, PACK], BF16, name=name, tag=tag, align_bytes=64)
             nc.vector.tensor_copy(
-                out=tile[:].rearrange("p (c i) j -> p c j i", i=4),
-                in_=raw[:].rearrange("p j (c i) -> p c j i", i=4),
+                out=tile[:].rearrange("p (c i) j -> p c j i", i=2),
+                in_=raw[:].rearrange("p j (c i) -> p c j i", i=2),
             )
             return tile
 
-        def quantise_weight(name, grouped):
-            codes = keep.tile([P, N], U32, name=name + "_codes", align_bytes=64)
+        def quantise_weight(name, grouped, tag):
+            codes = keep.tile([P, N], U32, name=name + "_codes", tag=tag, align_bytes=64)
             scales = keep.tile([P, N], U8, name=name + "_scales", align_bytes=64)
             nc.vector.quantize_mx(
                 out=codes[:].bitcast(FP8X4), scales=scales[:], in_=grouped[:].rearrange("p c j -> p (c j)")
@@ -130,19 +131,27 @@ def tile_picked_mixinhopggtan_none_p_kernel(
         for t in range(PACK):
             nc.gpsimd.memset(sig[t][:, S:], 0.0)
         w3_b = cast_weight("w3_b", w3_raw, "w3_b")
-        st = keep.tile([P, PACK, S], F32, name="st", tag="w3_raw")
+        st = keep.tile([P, PACK, S], F32, name="st")
         for t in range(PACK):
             nc.scalar.activation(out=sig[t][:, 0:S], in_=y_ps[t][:], func=ACT.Sigmoid)
             y_gain = keep.tile([P, S], F32, name="y_gain%d" % t, tag="y_gain%d" % t, align_bytes=64)
             nc.scalar.activation(out=y_gain[:], in_=y_ps[t][:], func=ACT.Copy, scale=gn_t[:, t : t + 1])
             nc.vector.tensor_tensor(out=st[:, t, :], in0=sig[t][:].indirect(n1_t[:]), in1=y_gain[:], op=ALU.mult)
             if t == 0:
-                w3_codes, w3_scales = quantise_weight("w3", w3_b)
+                w3_codes, w3_scales = quantise_weight("w3", w3_b, "w3_codes")
         w2_b = cast_weight("w2_b", w2_raw, "y_gain3")
-        w2_codes, w2_scales = quantise_weight("w2", w2_b)
 
+        w2_codes, w2_scales = quantise_weight("w2", w2_b, "w2_codes")
         z_codes = keep.tile([P, S], U32, name="z_codes", align_bytes=64)
         z_scales = keep.tile([P, S], U8, name="z_scales", align_bytes=64)
+        others = [keep.tile([P, PACK * HALF], F32, name="other%d" % a, tag="other%d" % a, align_bytes=64) for a in range(2)]
+        for a, t in [(0, 0), (0, 1), (0, 2), (1, 0), (0, 3), (1, 1), (1, 2), (1, 3)]:
+            if True:
+                nc.scalar.activation(
+                    out=others[a][:, t * HALF : (t + 1) * HALF],
+                    in_=st[:, t, :].indirect(n2_t[:, a * 16 : (a + 1) * 16]),
+                    func=ACT.Copy,
+                )
         h_ps = []
         for a in range(2):
             cols = slice(a * HALF, (a + 1) * HALF)
@@ -157,24 +166,21 @@ def tile_picked_mixinhopggtan_none_p_kernel(
                     out=banks[u][:],
                     lhsT=w3_codes[:, wc].bitcast(FP8X4),
                     lhsT_scale=w3_scales[:, wc],
-                    rhs=x2_words[:, cols].bitcast(FP8X4),
+                    rhs=x2_words[a][:].bitcast(FP8X4),
                     rhs_scale=x2_scales[:, cols],
                     start=True,
                     stop=False,
                 )
-            other = keep.tile([P, PACK * HALF], F32, name="other%d" % a)
+            other = others[a]
             for b0, b1 in [(0, HALF)]:
                 n = b1 - b0
                 c0 = a * HALF + b0
                 part = other[:, PACK * b0 : PACK * b1].rearrange("p (t c) -> p t c", t=PACK)
-                for t in range(PACK):
-                    src = st[:, t, :].indirect(n2_t[:, c0 // 16 : (c0 + n) // 16])
-                    nc.scalar.activation(out=part[:, t, :], in_=src, func=ACT.Copy)
-                z_b = keep.tile([P, n, PACK], BF16, name="z_b%d" % c0, tag="y_gain3", align_bytes=64)
+                z_b = keep.tile([P, n, PACK], BF16, name="z_b%d" % c0, align_bytes=64)
                 nc.vector.tensor_tensor(
-                    out=z_b[:].rearrange("p (c i) t -> p c t i", i=4),
-                    in0=st[:, :, c0 : c0 + n].rearrange("p t (c i) -> p c t i", i=4),
-                    in1=part.rearrange("p t (c i) -> p c t i", i=4),
+                    out=z_b[:].rearrange("p (c i) t -> p c t i", i=2),
+                    in0=st[:, :, c0 : c0 + n].rearrange("p t (c i) -> p c t i", i=2),
+                    in1=part.rearrange("p t (c i) -> p c t i", i=2),
                     op=ALU.subtract,
                 )
                 nc.vector.quantize_mx(
@@ -196,55 +202,43 @@ def tile_picked_mixinhopggtan_none_p_kernel(
         for u in range(4):
             nc.scalar.copy(out=h_sb[u][:, 0:HALF], in_=h_ps[0][u][:])
 
-        per = CHUNK // GROUP
-
         def copy_h(u, engine_copy):
             engine_copy(out=h_sb[u][:, HALF:S], in_=h_ps[1][u][:])
 
-        def finish(u, c0, c1, tag):
-            res = keep.tile([P, c1 - c0], F32, name="res%d_%d" % (u, c0), tag=tag)
-            nc.vector.tensor_tensor(out=res[:], in0=mx[u][:, c0:c1], in1=th[u][:, c0:c1], op=ALU.mult)
-            nc.sync.dma_start(out=out[u * P : (u + 1) * P, c0:c1], in_=res[:])
-
         mx = [keep.tile([P, S], F32, name="mx%d" % u) for u in range(4)]
         th = [keep.tile([P, S], F32, name="th%d" % u) for u in range(4)]
+        diff = [keep.tile([P, S], F32, name="diff%d" % u) for u in range(4)]
+        units = [(0, 0, 512, 0, [(0, 256, True), (256, 512, False)], [(0, 512)], []), (1, 0, 512, 1, [(0, 256, False), (256, 512, False)], [(0, 512)], [(0, 0, 512)]), (2, 0, 512, 2, [(0, 256, False), (256, 512, False)], [(0, 512)], [(1, 0, 512)]), (3, 0, 256, 3, [(0, 256, False)], [(0, 256)], []), (3, 256, 512, 3, [(256, 512, False)], [(256, 512)], [(2, 0, 512), (3, 0, 256), (3, 256, 512)])]
         copy_h(0, nc.vector.tensor_copy)
         copy_h(1, nc.scalar.copy)
-        for u in range(4):
-            mb = keep.tile([P, S, GROUP], F32, name="mb%d" % u, tag="mb%d" % u)
-            runs = ([(0, 1), (1, 2), (2, 3), (3, 4)], [(0, 2), (2, 4)], [(0, 2), (2, 4)], [(0, 2), (2, 3), (3, 4)])[u]
-            for g, g1 in runs:
-                dst = mb[:, g * per : g1 * per, :].rearrange("p j t -> p (j t)")
-                src = h_sb[u][:].indirect(n3_t[:, g * 32 : g1 * 32])
-                if u == 0 and g in (0, 2):
+        mbs = {}
+        for k, (u, c0, c1, mbk, vec, tanhs, results) in enumerate(units):
+            n = c1 - c0
+            if mbk not in mbs:
+                mbs[mbk] = (keep.tile([P, 512, GROUP], F32, name="mb%d" % mbk, tag="mb%d" % mbk), c0)
+            mb = mbs[mbk][0][:, c0 - mbs[mbk][1] : c1 - mbs[mbk][1], :]
+            for g0, g1, on_vector in vec:
+                dst = mb[:, g0 - c0 : g1 - c0, :].rearrange("p j t -> p (j t)")
+                src = h_sb[u][:].indirect(n3_t[:, g0 // 4 : g1 // 4])
+                if on_vector:
                     nc.vector.tensor_copy(out=dst, in_=src)
                 else:
                     nc.scalar.activation(out=dst, in_=src, func=ACT.Copy)
-            parts = [(0, 512)] if u < 3 else [(0, 256), (256, 384), (384, 512)]
-            for c0, c1 in parts:
-                n = c1 - c0
-                lo2 = ring.tile([P, n, 2], F32, name="lo2")
-                hi2 = ring.tile([P, n, 2], F32, name="hi2")
-                step = min(n, HALF)
-                for b0 in range(0, n, step):
-                    b1 = b0 + step
-                    src = mb[:, c0 + b0 : c0 + b1, :]
-                    nc.vector.tensor_tensor(out=lo2[:, b0:b1, :], in0=src[:, :, 0:2], in1=src[:, :, 2:4], op=ALU.min)
-                    nc.vector.tensor_tensor(out=hi2[:, b0:b1, :], in0=src[:, :, 0:2], in1=src[:, :, 2:4], op=ALU.max)
-                mn_tag = "mn%d_%d" % (u, c0)
-                mn = keep.tile([P, n], F32, name=mn_tag, tag=mn_tag)
-                nc.vector.tensor_tensor(out=mn[:], in0=lo2[:, :, 0], in1=lo2[:, :, 1], op=ALU.min)
-                nc.vector.tensor_tensor(out=mx[u][:, c0:c1], in0=hi2[:, :, 0], in1=hi2[:, :, 1], op=ALU.max)
-                diff_tag = "mb%d" % (u + 2) if u < 2 else "diff%d_%d" % (u, c0)
-                diff = keep.tile([P, n], F32, name="diff%d_%d" % (u, c0), tag=diff_tag)
-                nc.vector.tensor_tensor(out=diff[:], in0=h_sb[u][:, c0:c1], in1=mn[:], op=ALU.subtract)
-                nc.scalar.activation(out=th[u][:, c0:c1], in_=diff[:], func=ACT.Tanh)
-                if u in (1, 2):
-                    finish(u - 1, 0, S, mn_tag)
-                elif (u, c0) == (3, 256):
-                    finish(2, 0, S, mn_tag)
-                elif (u, c0) == (3, 384):
-                    finish(3, 0, 384, mn_tag)
-                    finish(3, 384, S, "res_last")
-            if u < 2:
-                copy_h(u + 2, nc.scalar.copy)
+            lo2 = keep.tile([P, n, 2], F32, name="lo%d" % k, tag="lo%d" % k)
+            hi2 = ring.tile([P, n, 2], F32, name="hi2")
+            for b0 in range(0, n, HALF):
+                b1 = min(n, b0 + HALF)
+                nc.vector.tensor_tensor(out=lo2[:, b0:b1], in0=mb[:, b0:b1, 0:2], in1=mb[:, b0:b1, 2:4], op=ALU.min)
+                nc.vector.tensor_tensor(out=hi2[:, b0:b1], in0=mb[:, b0:b1, 0:2], in1=mb[:, b0:b1, 2:4], op=ALU.max)
+            mn = keep.tile([P, n], F32, name="mn%d" % k, tag=("mb%d" % (k + 2) if k < 2 else "mn%d" % k))
+            nc.vector.tensor_tensor(out=mn[:], in0=lo2[:, :, 0], in1=lo2[:, :, 1], op=ALU.min)
+            nc.vector.tensor_tensor(out=mx[u][:, c0:c1], in0=hi2[:, :, 0], in1=hi2[:, :, 1], op=ALU.max)
+            nc.vector.tensor_tensor(out=diff[u][:, c0:c1], in0=h_sb[u][:, c0:c1], in1=mn[:], op=ALU.subtract)
+            for a0, a1 in tanhs:
+                nc.scalar.activation(out=th[u][:, a0:a1], in_=diff[u][:, a0:a1], func=ACT.Tanh)
+            for q, (ru, a0, a1) in enumerate(results):
+                res = keep.tile([P, a1 - a0], F32, name="res%d_%d" % (ru, a0), tag=("lo%d" % k if q == 0 else "res%d_%d" % (ru, a0)))
+                nc.vector.tensor_tensor(out=res[:], in0=mx[ru][:, a0:a1], in1=th[ru][:, a0:a1], op=ALU.mult)
+                nc.sync.dma_start(out=out[ru * P : (ru + 1) * P, a0:a1], in_=res[:])
+            if k in [0, 1]:
+                copy_h([0, 1].index(k) + 2, nc.vector.tensor_copy)

from contextlib import ExitStack

import concourse.mybir as mybir

K, T, S, N, H, W = 512, 2048, 512, 512, 512, 2048
FLOPS = 3 * 2 * 512 * 512 * 512

F32 = mybir.dt.float32
BF16 = mybir.dt.bfloat16
I32 = mybir.dt.int32
U32 = mybir.dt.uint32
U16 = mybir.dt.uint16
U8 = mybir.dt.uint8
FP8X4 = mybir.dt.float8_e4m3fn_x4
ALU = mybir.AluOpType
ACT = mybir.ActivationFunctionType

P = 128
PACK = 4
SPARE = 16
HALF = S // 2
GROUP = 4
CHUNK = 512


def tile_picked_mixinhopggtan_none_p_kernel(
    tc, x_words, x_scales, w1, gn, w2, w3, offs, n1, n2, two, n3, out
):
    nc = tc.nc
    with ExitStack() as ctx:
        keep = ctx.enter_context(tc.tile_pool(name="keep", bufs=1))
        ring = ctx.enter_context(tc.tile_pool(name="ring", bufs=2))
        psum = ctx.enter_context(tc.psum_pool(name="psum", bufs=1))

        def load_list(name, src):
            tile = keep.tile(list(src.shape), U16, name=name)
            nc.sync.dma_start(out=tile[:], in_=src)
            return tile

        xs = keep.tile([P, T], U8, name="xs", align_bytes=64)
        offs_t = load_list("offs_t", offs)
        for q in range(4):
            nc.sync.dma_start(
                out=xs[32 * q : 32 * q + 32, :].bitcast(I32),
                in_=x_scales[0, 4 * q : 4 * q + 4, :].bitcast(I32).unsqueeze(0).broadcast_to([8, 4, T // 4]),
            )
        two_t = load_list("two_t", two)
        xw = keep.tile([P, T], U32, name="xw", align_bytes=64)
        nc.sync.dma_start(
            out=xw[:].bitcast(I32),
            in_=x_words[0].rearrange("p n r -> p (n r)").bitcast(I32),
        )
        w1_rows = w1.rearrange("(p j) c -> p j c", j=PACK)
        w1_raw = []
        for a in range(2):
            raw = keep.tile([P, PACK, H // 2], F32, name="w1_raw%d" % a)
            nc.sync.dma_start(out=raw[:], in_=w1_rows[:, :, a * (H // 2) : (a + 1) * (H // 2)])
            w1_raw.append(raw)
        n1_t = load_list("n1_t", n1)
        gn_t = keep.tile([P, PACK], F32, name="gn_t")
        nc.sync.dma_start(out=gn_t[:], in_=gn.rearrange("(p t) o -> p (t o)", t=PACK))
        w3_raw = keep.tile([P, PACK, N], F32, name="w3_raw", tag="w3_raw")
        nc.sync.dma_start(out=w3_raw[:], in_=w3.rearrange("(p j) c -> p j c", j=PACK))
        n2_t = load_list("n2_t", n2)
        w2_raw = keep.tile([P, PACK, N], F32, name="w2_raw")
        nc.sync.dma_start(out=w2_raw[:], in_=w2.rearrange("(p j) c -> p j c", j=PACK))
        n3_t = load_list("n3_t", n3)

        h_sb = [keep.tile([P, 2 * S + SPARE], F32, name="h_sb%d" % u) for u in range(4)]
        for u in range(4):
            nc.gpsimd.memset(h_sb[u][:, S:], 0.0)

        def pick(name, window, offsets, dtype, tag=None):
            tile = keep.tile([P, offsets.shape[1] * 16], dtype, name=name, tag=tag or name, align_bytes=64)
            nc.vector.tensor_copy(out=tile[:], in_=window[:].indirect(offsets))
            return tile

        xq_scales = pick("xq_scales", xs, offs_t[:], U8)
        x2_scales = pick("x2_scales", xs, two_t[:], U8)
        xq_words = pick("xq_words", xw, offs_t[:], U32)

        w1_b = keep.tile([P, PACK, P, PACK], BF16, name="w1_b", tag="w1_b", align_bytes=64)
        w1_view = w1_b[:].rearrange("p t m j -> p m j t")
        nc.scalar.copy(
            out=w1_view[:, 0 : P // 2], in_=w1_raw[0][:].rearrange("p j (m t) -> p m j t", t=PACK)
        )
        x2_words = [pick("x2_words0", xw, two_t[:, 0:16], U32)]
        nc.vector.tensor_copy(
            out=w1_view[:, P // 2 : P], in_=w1_raw[1][:].rearrange("p j (m t) -> p m j t", t=PACK)
        )
        w1_codes = keep.tile([P, H], U32, name="w1_codes", align_bytes=64)
        w1_scales = keep.tile([P, H], U8, name="w1_scales", align_bytes=64)
        y_ps = [psum.tile([P, S], F32, name="y_ps%d" % t, tag="y_ps%d" % t) for t in range(PACK)]
        for t0, t1 in ((0, 1), (1, PACK)):
            cols = slice(t0 * P, t1 * P)
            nc.vector.quantize_mx(
                out=w1_codes[:, cols].bitcast(FP8X4),
                scales=w1_scales[:, cols],
                in_=w1_b[:, t0:t1].rearrange("p t m j -> p (t m j)"),
            )
        x2_words.append(pick("x2_words1", xw, two_t[:, 16:32], U32, tag="w1_b"))
        for t in range(PACK):
            cols = slice(t * P, (t + 1) * P)
            nc.tensor.matmul_mx(
                out=y_ps[t][:],
                lhsT=w1_codes[:, cols].bitcast(FP8X4),
                lhsT_scale=w1_scales[:, cols],
                rhs=xq_words[:].bitcast(FP8X4),
                rhs_scale=xq_scales[:],
                start=True,
                stop=True,
            )

        def cast_weight(name, raw, tag):
            tile = keep.tile([P, N, PACK], BF16, name=name, tag=tag, align_bytes=64)
            nc.vector.tensor_copy(
                out=tile[:].rearrange("p (c i) j -> p c j i", i=2),
                in_=raw[:].rearrange("p j (c i) -> p c j i", i=2),
            )
            return tile

        def quantise_weight(name, grouped, tag):
            codes = keep.tile([P, N], U32, name=name + "_codes", tag=tag, align_bytes=64)
            scales = keep.tile([P, N], U8, name=name + "_scales", align_bytes=64)
            nc.vector.quantize_mx(
                out=codes[:].bitcast(FP8X4), scales=scales[:], in_=grouped[:].rearrange("p c j -> p (c j)")
            )
            return codes, scales

        sig = [keep.tile([P, S + SPARE], F32, name="sig%d" % t) for t in range(PACK)]
        for t in range(PACK):
            nc.gpsimd.memset(sig[t][:, S:], 0.0)
        w3_b = cast_weight("w3_b", w3_raw, "w3_b")
        st = keep.tile([P, PACK, S], F32, name="st")
        for t in range(PACK):
            nc.scalar.activation(out=sig[t][:, 0:S], in_=y_ps[t][:], func=ACT.Sigmoid)
            y_gain = keep.tile([P, S], F32, name="y_gain%d" % t, tag="y_gain%d" % t, align_bytes=64)
            nc.scalar.activation(out=y_gain[:], in_=y_ps[t][:], func=ACT.Copy, scale=gn_t[:, t : t + 1])
            nc.vector.tensor_tensor(out=st[:, t, :], in0=sig[t][:].indirect(n1_t[:]), in1=y_gain[:], op=ALU.mult)
            if t == 0:
                w3_codes, w3_scales = quantise_weight("w3", w3_b, "w3_codes")
        w2_b = cast_weight("w2_b", w2_raw, "y_gain3")

        w2_codes, w2_scales = quantise_weight("w2", w2_b, "w2_codes")
        z_codes = keep.tile([P, S], U32, name="z_codes", align_bytes=64)
        z_scales = keep.tile([P, S], U8, name="z_scales", align_bytes=64)
        others = [keep.tile([P, PACK * HALF], F32, name="other%d" % a, tag="other%d" % a, align_bytes=64) for a in range(2)]
        for a, t in [(0, 0), (0, 1), (0, 2), (1, 0), (0, 3), (1, 1), (1, 2), (1, 3)]:
            if True:
                nc.scalar.activation(
                    out=others[a][:, t * HALF : (t + 1) * HALF],
                    in_=st[:, t, :].indirect(n2_t[:, a * 16 : (a + 1) * 16]),
                    func=ACT.Copy,
                )
        h_ps = []
        for a in range(2):
            cols = slice(a * HALF, (a + 1) * HALF)
            banks = [
                psum.tile([P, HALF], F32, name="h_ps%d_%d" % (a, u), tag=("h_ps%d", "y_ps%d")[a] % u)
                for u in range(4)
            ]
            h_ps.append(banks)
            for u in range(4):
                wc = slice(u * P, (u + 1) * P)
                nc.tensor.matmul_mx(
                    out=banks[u][:],
                    lhsT=w3_codes[:, wc].bitcast(FP8X4),
                    lhsT_scale=w3_scales[:, wc],
                    rhs=x2_words[a][:].bitcast(FP8X4),
                    rhs_scale=x2_scales[:, cols],
                    start=True,
                    stop=False,
                )
            other = others[a]
            for b0, b1 in [(0, HALF)]:
                n = b1 - b0
                c0 = a * HALF + b0
                part = other[:, PACK * b0 : PACK * b1].rearrange("p (t c) -> p t c", t=PACK)
                z_b = keep.tile([P, n, PACK], BF16, name="z_b%d" % c0, align_bytes=64)
                nc.vector.tensor_tensor(
                    out=z_b[:].rearrange("p (c i) t -> p c t i", i=2),
                    in0=st[:, :, c0 : c0 + n].rearrange("p t (c i) -> p c t i", i=2),
                    in1=part.rearrange("p t (c i) -> p c t i", i=2),
                    op=ALU.subtract,
                )
                nc.vector.quantize_mx(
                    out=z_codes[:, c0 : c0 + n].bitcast(FP8X4),
                    scales=z_scales[:, c0 : c0 + n],
                    in_=z_b[:].rearrange("p c t -> p (c t)"),
                )
                for u in range(4):
                    wc = slice(u * P, (u + 1) * P)
                    nc.tensor.matmul_mx(
                        out=banks[u][:, b0:b1],
                        lhsT=w2_codes[:, wc].bitcast(FP8X4),
                        lhsT_scale=w2_scales[:, wc],
                        rhs=z_codes[:, c0 : c0 + n].bitcast(FP8X4),
                        rhs_scale=z_scales[:, c0 : c0 + n],
                        start=False,
                        stop=(b1 == HALF),
                    )
        for u in range(4):
            nc.scalar.copy(out=h_sb[u][:, 0:HALF], in_=h_ps[0][u][:])

        def copy_h(u, engine_copy):
            engine_copy(out=h_sb[u][:, HALF:S], in_=h_ps[1][u][:])

        mx = [keep.tile([P, S], F32, name="mx%d" % u) for u in range(4)]
        th = [keep.tile([P, S], F32, name="th%d" % u) for u in range(4)]
        diff = [keep.tile([P, S], F32, name="diff%d" % u) for u in range(4)]
        units = [(0, 0, 512, 0, [(0, 256, True), (256, 512, False)], [(0, 512)], []), (1, 0, 512, 1, [(0, 256, False), (256, 512, False)], [(0, 512)], [(0, 0, 512)]), (2, 0, 512, 2, [(0, 256, False), (256, 512, False)], [(0, 512)], [(1, 0, 512)]), (3, 0, 256, 3, [(0, 256, False)], [(0, 256)], []), (3, 256, 512, 3, [(256, 512, False)], [(256, 512)], [(2, 0, 512), (3, 0, 256), (3, 256, 512)])]
        copy_h(0, nc.vector.tensor_copy)
        copy_h(1, nc.scalar.copy)
        mbs = {}
        for k, (u, c0, c1, mbk, vec, tanhs, results) in enumerate(units):
            n = c1 - c0
            if mbk not in mbs:
                mbs[mbk] = (keep.tile([P, 512, GROUP], F32, name="mb%d" % mbk, tag="mb%d" % mbk), c0)
            mb = mbs[mbk][0][:, c0 - mbs[mbk][1] : c1 - mbs[mbk][1], :]
            for g0, g1, on_vector in vec:
                dst = mb[:, g0 - c0 : g1 - c0, :].rearrange("p j t -> p (j t)")
                src = h_sb[u][:].indirect(n3_t[:, g0 // 4 : g1 // 4])
                if on_vector:
                    nc.vector.tensor_copy(out=dst, in_=src)
                else:
                    nc.scalar.activation(out=dst, in_=src, func=ACT.Copy)
            lo2 = keep.tile([P, n, 2], F32, name="lo%d" % k, tag="lo%d" % k)
            hi2 = ring.tile([P, n, 2], F32, name="hi2")
            for b0 in range(0, n, HALF):
                b1 = min(n, b0 + HALF)
                nc.vector.tensor_tensor(out=lo2[:, b0:b1], in0=mb[:, b0:b1, 0:2], in1=mb[:, b0:b1, 2:4], op=ALU.min)
                nc.vector.tensor_tensor(out=hi2[:, b0:b1], in0=mb[:, b0:b1, 0:2], in1=mb[:, b0:b1, 2:4], op=ALU.max)
            mn = keep.tile([P, n], F32, name="mn%d" % k, tag=("mb%d" % (k + 2) if k < 2 else "mn%d" % k))
            nc.vector.tensor_tensor(out=mn[:], in0=lo2[:, :, 0], in1=lo2[:, :, 1], op=ALU.min)
            nc.vector.tensor_tensor(out=mx[u][:, c0:c1], in0=hi2[:, :, 0], in1=hi2[:, :, 1], op=ALU.max)
            nc.vector.tensor_tensor(out=diff[u][:, c0:c1], in0=h_sb[u][:, c0:c1], in1=mn[:], op=ALU.subtract)
            for a0, a1 in tanhs:
                nc.scalar.activation(out=th[u][:, a0:a1], in_=diff[u][:, a0:a1], func=ACT.Tanh)
            for q, (ru, a0, a1) in enumerate(results):
                res = keep.tile([P, a1 - a0], F32, name="res%d_%d" % (ru, a0), tag=("lo%d" % k if q == 0 else "res%d_%d" % (ru, a0)))
                nc.vector.tensor_tensor(out=res[:], in0=mx[ru][:, a0:a1], in1=th[ru][:, a0:a1], op=ALU.mult)
                nc.sync.dma_start(out=out[ru * P : (ru + 1) * P, a0:a1], in_=res[:])
            if k in [0, 1]:
                copy_h([0, 1].index(k) + 2, nc.vector.tensor_copy)
